import numpy as np
import ml_dtypes


def mxq(x, axis, fmt="e4m3"):
    dtype, down = {"e4m3": (ml_dtypes.float8_e4m3fn, 7), "e5m2": (ml_dtypes.float8_e5m2, 14)}[fmt]
    v = np.moveaxis(np.asarray(x, np.float32).astype(ml_dtypes.bfloat16).astype(np.float64), axis, -1)
    blocks = v.reshape(v.shape[:-1] + (-1, 32))
    amax = np.abs(blocks).max(-1, keepdims=True)
    byte = np.maximum(np.where(amax > 0, np.frexp(amax)[1] - 1 + 127, 0) - down, 1)
    scale = np.exp2(byte - 127.0)
    codes = (blocks / scale).astype(np.float32).astype(dtype).astype(np.float64)
    return np.moveaxis((codes * scale).reshape(v.shape), -1, axis)


WIDE = False


def mx_kscale(k):
    if not WIDE:
        return np.ones(k)
    levels = np.array([30, -30])
    if k % 512:
        return np.exp2(np.random.permutation(np.resize(levels, k // 32))).repeat(32)
    a = np.empty((k // 512, 16))
    for p in range(k // 512):
        a[p, :8] = np.random.permutation(np.resize(levels, 8))
        for g in range(8):
            far = levels[np.abs(levels - a[p, g]) >= 10]
            a[p, g + 8] = far[np.random.randint(len(far))]
    return np.exp2(a.ravel()).repeat(32)


def f64(x):
    return np.asarray(x).astype(np.float64)


def striped(idx):
    return np.tile(np.asarray(idx).reshape(-1, 16).T, (8, 1)).astype(np.uint16)


def unstriped(offs):
    return offs[:16].T.reshape(-1).astype(np.int64)


E2M1 = np.array([0.0, 0.5, 1.0, 1.5, 2.0, 3.0, 4.0, 6.0, -0.0, -0.5, -1.0, -1.5, -2.0, -3.0, -4.0, -6.0])


def pack_weight(w, fmt):
    k, n = w.shape
    w = f64(np.asarray(w, np.float32).astype(ml_dtypes.bfloat16)).reshape(k // 32, 32, n)
    amax = np.abs(w).max(1)
    if fmt in ("e4m3", "e5m2"):
        byte = np.frexp(amax)[1] - 1 + 127 - (7 if fmt == "e4m3" else 14)
    else:
        mant, ex = np.frexp(amax / 6.0)
        byte = np.where(mant > 0.5, ex, ex - 1) + 127
    byte = np.clip(np.where(amax > 0, byte, 1), 1, 254)
    scaled = (w * np.exp2(127.0 - byte)[:, None, :]).reshape(k, n).astype(np.float32)
    by_word = np.ascontiguousarray(scaled.reshape(k // 512, 128, 4, n).transpose(0, 1, 3, 2))
    if fmt in ("e4m3", "e5m2"):
        words = by_word.astype(ml_dtypes.float8_e4m3fn if fmt == "e4m3" else ml_dtypes.float8_e5m2).view(np.uint8)
    else:
        c = by_word.astype(ml_dtypes.float4_e2m1fn).view(np.uint8) & 0xF
        words = (c[..., 0::2] | (c[..., 1::2] << 4)).reshape(k // 512, 128, 2 * n)
    return np.ascontiguousarray(words), np.ascontiguousarray(byte.astype(np.uint8).reshape(k // 512, 16, n))


def unpack_weight(words, scales, fmt):
    g, _, n = scales.shape
    words = np.ascontiguousarray(words).reshape(g, 128, n, -1)
    if fmt in ("e4m3", "e5m2"):
        vals = words.view(ml_dtypes.float8_e4m3fn if fmt == "e4m3" else ml_dtypes.float8_e5m2).astype(np.float64)
    else:
        nib = np.empty((g, 128, n, 4), np.uint8)
        nib[..., 0::2] = words & 0xF
        nib[..., 1::2] = words >> 4
        vals = E2M1[nib]
    vals = vals * np.repeat(np.exp2(scales.astype(np.float64) - 127.0), 8, axis=1)[..., None]
    return vals.transpose(0, 1, 3, 2).reshape(g * 512, n)


K, T, J, R, V, M, Q, O, D, N, U = 512, 1024, 256, 512, 1024, 512, 128, 128, 256, 256, 128


def setup_inputs():
    n = np.random.standard_normal
    idx = np.random.permutation(V)[:R]
    idx2 = np.random.permutation(T)[:J]
    idx3 = np.random.permutation(J)[:O]
    idx4 = np.random.permutation(J)[:O]
    idx5 = np.random.permutation(D)[:U]
    idx6 = np.random.permutation(D)[:U]
    fk = mx_kscale(K)
    fm = mx_kscale(M)
    fr = mx_kscale(R)
    xtp = pack_weight(n((K, T)) / fk[:, None], "e4m3")
    wtp = pack_weight(n((K, V)) * 1 / np.sqrt(K) * fk[:, None], "e2m1")
    xcp = pack_weight(n((M, Q)) / fm[:, None], "e4m3")
    wgp = pack_weight(n((M, R)) * 1 / np.sqrt(M) * fm[:, None] * fr, "e2m1")
    wbp = pack_weight(n((R, N)) * 1 / np.sqrt(R) / fr[:, None], "e5m2")
    return {
        "xt_words": xtp[0],
        "xt_scales": xtp[1],
        "wt_words": wtp[0],
        "wt_scales": wtp[1],
        "xc_words": xcp[0],
        "xc_scales": xcp[1],
        "wg_words": wgp[0],
        "wg_scales": wgp[1],
        "wb_words": wbp[0],
        "wb_scales": wbp[1],
        "so": (np.random.uniform(0.5, 1.6, (N, 1))).astype(np.float32),
        "offs": striped(idx),
        "offs2": striped(idx2),
        "offs3": striped(idx3),
        "offs4": striped(idx4),
        "offs5": striped(idx5),
        "offs6": striped(idx6),
    }


def reference(xt_words, xt_scales, wt_words, wt_scales, xc_words, xc_scales, wg_words, wg_scales, wb_words, wb_scales, so, offs, offs2, offs3, offs4, offs5, offs6):
    idx = unstriped(offs)
    idx2 = unstriped(offs2)
    idx3 = unstriped(offs3)
    idx4 = unstriped(offs4)
    idx5 = unstriped(offs5)
    idx6 = unstriped(offs6)
    xtu = unpack_weight(xt_words, xt_scales, "e4m3")
    wtu = unpack_weight(wt_words, wt_scales, "e2m1")
    xcu = unpack_weight(xc_words, xc_scales, "e4m3")
    wgu = unpack_weight(wg_words, wg_scales, "e2m1")
    wbu = unpack_weight(wb_words, wb_scales, "e5m2")
    wtidxg = wtu[:, idx]
    xtidx2g = xtu[:, idx2]
    a = wtidxg.T @ xtidx2g
    g0 = wgu.T @ xcu
    ga = g0[:, 0:1]
    gb = g0[:, 64:65]
    h1 = np.maximum(a[:, idx3] * ga, a[:, idx4] * gb)
    hid = np.concatenate([h1, g0], axis=1)
    hidq = mxq(hid, 0, "e4m3")
    p = wbu.T @ hidq
    y = p[:, idx5] - p[:, idx6] * f64(so)
    return y

@@ -1,0 +1,183 @@
+from contextlib import ExitStack
+
+import concourse.mybir as mybir
+from concourse.masks import make_identity
+
+F32 = mybir.dt.float32
+BF16 = mybir.dt.bfloat16
+I32 = mybir.dt.int32
+U32 = mybir.dt.uint32
+U16 = mybir.dt.uint16
+U8 = mybir.dt.uint8
+E4M3 = mybir.dt.float8_e4m3fn_x4
+E5M2 = mybir.dt.float8_e5m2_x4
+E2M1 = mybir.dt.float4_e2m1fn_x4
+COPY = mybir.ActivationFunctionType.Copy
+ALU = mybir.AluOpType
+
+P = 128
+PACK = 4
+T, J, R, V, Q, O, D, N, U = 1024, 256, 512, 1024, 128, 128, 256, 256, 128
+FLOPS = 2 * 512 * (R * J + R * Q + N * D)
+
+
+def tile_list_ctxbeside_chosen_one_weighedout_kernel(
+    tc, xt_words, xt_scales, wt_words, wt_scales, xc_words, xc_scales, wg_words, wg_scales,
+    wb_words, wb_scales, so, offs, offs2, offs3, offs4, offs5, offs6, out
+):
+    nc = tc.nc
+    with ExitStack() as ctx:
+        sb = ctx.enter_context(tc.tile_pool(name="sb", bufs=1))
+        ps = ctx.enter_context(tc.psum_pool(name="ps", bufs=1))
+
+        def load_list(name, src):
+            tile = sb.tile(list(src.shape), U16, name=name)
+            nc.sync.dma_start(tile[:], src)
+            return tile
+
+        def load_words(queue, name, src, dtype, cols):
+            tile = sb.tile([P, cols], dtype, name=name, align_bytes=64)
+            rows = src[0] if src.ndim == 3 else src[0].rearrange("p n t -> p (n t)")
+            queue.dma_start(tile[:].bitcast(I32), rows.bitcast(I32))
+            return tile
+
+        def zeroed_plane(name, cols):
+            tile = sb.tile([P, cols], U8, name=name, align_bytes=64)
+            nc.vector.memset(tile[:].bitcast(I32), 0)
+            return tile
+
+        def load_scales(plane, src):
+            rows = src[0].bitcast(I32)
+            for quad in range(4):
+                nc.sync.dma_start(plane[32 * quad : 32 * quad + 4, :].bitcast(I32), rows[4 * quad : 4 * quad + 4, :])
+
+        g_plane = zeroed_plane("g_plane", R + Q)
+        wt_s = zeroed_plane("wt_s", V)
+        xt_s = zeroed_plane("xt_s", T)
+        wb_s = zeroed_plane("wb_s", N)
+
+        staged = sb.tile([4, 4, (R + Q) // 4], I32)
+        nc.sync.dma_start(staged[:, :, 0 : R // 4], wg_scales[0].bitcast(I32).rearrange("(q r) c -> r q c", r=4))
+        wt_w = load_words(nc.scalar, "wt_w", wt_words, U16, V)
+        nc.sync.dma_start(staged[:, :, R // 4 :], xc_scales[0].bitcast(I32).rearrange("(q r) c -> r q c", r=4))
+        wg_w = load_words(nc.scalar, "wg_w", wg_words, U16, R)
+        l1 = load_list("l1", offs)
+        xc_w = load_words(nc.scalar, "xc_w", xc_words, U32, Q)
+        l2 = load_list("l2", offs2)
+        xt_w = load_words(nc.scalar, "xt_w", xt_words, U32, T)
+        load_scales(wt_s, wt_scales)
+        load_scales(xt_s, xt_scales)
+        l3 = load_list("l3", offs3)
+        l4 = load_list("l4", offs4)
+        wb_w = load_words(nc.sync, "wb_w", wb_words, U32, N)
+        load_scales(wb_s, wb_scales)
+        l5 = load_list("l5", offs5)
+        l6 = load_list("l6", offs6)
+        for quad in range(4):
+            nc.vector.tensor_copy(g_plane[32 * quad : 32 * quad + 4, :].bitcast(I32), staged[:, quad, :])
+        wg_s = g_plane[:, 0:R]
+        xc_s = g_plane[:, R : R + Q]
+        so_t = sb.tile([P, 2], F32)
+        with nc.allow_non_contiguous_dma(reason="one weight a partition"):
+            nc.sync.dma_start(so_t[:], so.rearrange("(h p) o -> p (h o)", p=P))
+
+        ident = sb.tile([P, P], F32)
+        make_identity(nc, ident[:])
+
+        wt_gw = sb.tile([P, R], U16, align_bytes=64)
+        nc.vector.tensor_copy(wt_gw[:], wt_w[:].indirect(l1[:]))
+        xt_gw = sb.tile([P, J], U32, align_bytes=64)
+        nc.vector.tensor_copy(xt_gw[:], xt_w[:].indirect(l2[:]))
+        wt_dw = sb.tile([P, PACK, P], U16, align_bytes=64)
+        nc.vector.tensor_copy(
+            wt_dw[:].rearrange("p t (c i) -> p c t i", i=8),
+            wt_gw[:].rearrange("p (c i t) -> p c t i", i=8, t=PACK),
+        )
+        wt_gs = sb.tile([P, PACK, P], U8, align_bytes=64)
+        nc.vector.tensor_copy(wt_gs[:].rearrange("p t m -> p m t"), wt_s[:].indirect(l1[:]))
+        xt_gs = sb.tile([P, J], U8, align_bytes=64)
+        nc.vector.tensor_copy(xt_gs[:], xt_s[:].indirect(l2[:]))
+
+        gT_ps = ps.tile([P, R], F32, tag="shared")
+        nc.tensor.matmul_mx(out=gT_ps[:], lhsT=xc_w[:].bitcast(E4M3), lhsT_scale=xc_s,
+                            rhs=wg_w[:].bitcast(E2M1), rhs_scale=wg_s, start=True, stop=True)
+        gT = sb.tile([P, PACK, P], F32)
+        nc.scalar.activation(gT[:], gT_ps[:].rearrange("q (m t) -> q t m", t=PACK), COPY)
+        g_ps = ps.tile([P, PACK, Q], F32)
+        for t in range(PACK):
+            nc.tensor.transpose(g_ps[:, t, :], gT[:, t, :], ident[:])
+        g0 = sb.tile([P, PACK, Q], F32)
+        nc.scalar.activation(g0[:], g_ps[:], COPY)
+        hid_g = sb.tile([P, Q, PACK], BF16, align_bytes=64)
+        nc.scalar.activation(hid_g[:], g_ps[:].rearrange("p t q -> p q t"), COPY)
+
+        a = []
+        for t in range(PACK):
+            a_ps = ps.tile([P, J], F32, name=f"a_ps{t}")
+            nc.tensor.matmul_mx(out=a_ps[:], lhsT=wt_dw[:, t, :].bitcast(E2M1), lhsT_scale=wt_gs[:, t, :],
+                                rhs=xt_gw[:].bitcast(E4M3), rhs_scale=xt_gs[:], start=True, stop=True)
+            a_t = sb.tile([P, J], F32, name=f"a{t}")
+            nc.vector.tensor_copy(a_t[:], a_ps[:])
+            a.append(a_t)
+
+        g_w = sb.tile([P, Q], U32, align_bytes=64)
+        g_s = sb.tile([P, Q], U8, align_bytes=64)
+        nc.vector.quantize_mx(out=g_w[:].bitcast(E4M3), scales=g_s[:], in_=hid_g[:].rearrange("p q t -> p (q t)"))
+        p_sb = [sb.tile([P, D], F32, name=f"p{h}") for h in range(2)]
+        pg_ps = ps.tile([P, 2, Q], F32, tag="shared")
+        for h in range(2):
+            cols = slice(h * P, (h + 1) * P)
+            nc.tensor.matmul_mx(out=pg_ps[:, h, :], lhsT=wb_w[:, cols].bitcast(E5M2), lhsT_scale=wb_s[:, cols],
+                                rhs=g_w[:].bitcast(E4M3), rhs_scale=g_s[:], start=True, stop=True)
+        for h in range(2):
+            nc.vector.tensor_copy(p_sb[h][:, O:D], pg_ps[:, h, :])
+
+        first = sb.tile([P, PACK, O], F32)
+        second = sb.tile([P, PACK, O], F32)
+        hid_h = sb.tile([P, O, PACK], BF16, align_bytes=64)
+        h_w = sb.tile([P, O], U32, align_bytes=64)
+        h_s = sb.tile([P, O], U8, align_bytes=64)
+
+        def fetch(t, lo, hi):
+            cols = slice(lo // 16, hi // 16)
+            nc.scalar.activation(first[:, t, lo:hi], a[t][:].indirect(l3[:, cols]), COPY, scale=g0[:, t, 0:1])
+            nc.scalar.activation(second[:, t, lo:hi], a[t][:].indirect(l4[:, cols]), COPY, scale=g0[:, t, 64:65])
+
+        def larger(t, lo, hi):
+            nc.vector.tensor_tensor(
+                hid_h[:, lo:hi, t : t + 2],
+                first[:, t : t + 2, lo:hi].rearrange("p t o -> p o t"),
+                second[:, t : t + 2, lo:hi].rearrange("p t o -> p o t"),
+                ALU.max,
+            )
+
+        fetch(0, 0, O)
+        fetch(1, 0, O)
+        larger(0, 0, O)
+        halves = [(0, O // 2), (O // 2, O)]
+        for lo, hi in halves:
+            fetch(2, lo, hi)
+            fetch(3, lo, hi)
+            larger(2, lo, hi)
+        for lo, hi in halves:
+            nc.vector.quantize_mx(out=h_w[:, lo:hi].bitcast(E4M3), scales=h_s[:, lo:hi],
+                                  in_=hid_h[:, lo:hi, :].rearrange("p o t -> p (o t)"))
+
+        for h in range(2):
+            cols = slice(h * P, (h + 1) * P)
+            ph_ps = ps.tile([P, O], F32, name=f"ph_ps{h}")
+            nc.tensor.matmul_mx(out=ph_ps[:], lhsT=wb_w[:, cols].bitcast(E5M2), lhsT_scale=wb_s[:, cols],
+                                rhs=h_w[:].bitcast(E4M3), rhs_scale=h_s[:], start=True, stop=True)
+            if h == 0:
+                nc.vector.tensor_copy(p_sb[h][:, 0:O], ph_ps[:])
+            else:
+                nc.scalar.activation(p_sb[h][:, 0:O], ph_ps[:], COPY)
+        weighed = [sb.tile([P, U], F32, name=f"weighed{h}") for h in range(2)]
+        kept = [sb.tile([P, U], F32, name=f"kept{h}") for h in range(2)]
+        for h in range(2):
+            nc.scalar.activation(weighed[h][:], p_sb[h][:].indirect(l6[:]), COPY, scale=so_t[:, h : h + 1])
+            nc.vector.tensor_copy(kept[h][:], p_sb[h][:].indirect(l5[:]))
+        for h in range(2):
+            y = sb.tile([P, U], F32, name=f"y{h}")
+            nc.vector.tensor_tensor(y[:], kept[h][:], weighed[h][:], ALU.subtract)
+            (nc.scalar if h == 0 else nc.sync).dma_start(out[h * P : (h + 1) * P, :], y[:])

@@ -88,15 +88,23 @@ def tile_list_ctxbeside_chosen_one_weighedout_kernel(
         nc.vector.tensor_copy(wt_gw[:], wt_w[:].indirect(l1[:]))
         xt_gw = sb.tile([P, J], U32, align_bytes=64)
         nc.vector.tensor_copy(xt_gw[:], xt_w[:].indirect(l2[:]))
-        wt_dw = sb.tile([P, PACK, P], U16, align_bytes=64)
-        nc.vector.tensor_copy(
-            wt_dw[:].rearrange("p t (c i) -> p c t i", i=8),
-            wt_gw[:].rearrange("p (c i t) -> p c t i", i=8, t=PACK),
-        )
+
+        def deal(t, tag):
+            tile = sb.tile([P, 2, P], U16, name=f"wt_dw{t}", tag=tag, align_bytes=64)
+            nc.vector.tensor_copy(
+                tile[:].rearrange("p t (c i) -> p c t i", i=8),
+                wt_gw[:].rearrange("p (c i t) -> p c t i", i=8, t=PACK)[:, :, t : t + 2, :],
+            )
+            return [tile[:, 0, :], tile[:, 1, :]]
+
+        wt_dw = deal(0, "wt_dw")
         wt_gs = sb.tile([P, PACK, P], U8, align_bytes=64)
         nc.vector.tensor_copy(wt_gs[:].rearrange("p t m -> p m t"), wt_s[:].indirect(l1[:]))
         xt_gs = sb.tile([P, J], U8, align_bytes=64)
-        nc.vector.tensor_copy(xt_gs[:], xt_s[:].indirect(l2[:]))
+        for lo in (0, J // 2):
+            nc.vector.tensor_copy(xt_gs[:, lo : lo + J // 2], xt_s[:].indirect(l2[:, lo // 16 : (lo + J // 2) // 16]))
+
+        wt_dw = wt_dw + deal(2, "xt_s")
 
         gT_ps = ps.tile([P, R], F32, tag="shared")
         nc.tensor.matmul_mx(out=gT_ps[:], lhsT=xc_w[:].bitcast(E4M3), lhsT_scale=xc_s,
@@ -111,14 +119,18 @@ def tile_list_ctxbeside_chosen_one_weighedout_kernel(
         hid_g = sb.tile([P, Q, PACK], BF16, align_bytes=64)
         nc.scalar.activation(hid_g[:], g_ps[:].rearrange("p t q -> p q t"), COPY)
 
-        a = []
-        for t in range(PACK):
-            a_ps = ps.tile([P, J], F32, name=f"a_ps{t}")
-            nc.tensor.matmul_mx(out=a_ps[:], lhsT=wt_dw[:, t, :].bitcast(E2M1), lhsT_scale=wt_gs[:, t, :],
-                                rhs=xt_gw[:].bitcast(E4M3), rhs_scale=xt_gs[:], start=True, stop=True)
-            a_t = sb.tile([P, J], F32, name=f"a{t}")
-            nc.vector.tensor_copy(a_t[:], a_ps[:])
-            a.append(a_t)
+        a = [sb.tile([P, J], F32, name=f"a{t}") for t in range(PACK)]
+
+        def hidden(t, lo, hi, bank, copy):
+            a_ps = ps.tile([P, hi - lo], F32, name=bank)
+            nc.tensor.matmul_mx(out=a_ps[:], lhsT=wt_dw[t].bitcast(E2M1), lhsT_scale=wt_gs[:, t, :],
+                                rhs=xt_gw[:, lo:hi].bitcast(E4M3), rhs_scale=xt_gs[:, lo:hi], start=True, stop=True)
+            copy(a[t][:, lo:hi], a_ps[:])
+
+        hidden(0, 0, J // 2, "bank_a", nc.scalar.copy)
+        hidden(0, J // 2, J, "bank_b", nc.vector.tensor_copy)
+        for t in range(1, PACK):
+            hidden(t, 0, J, f"a_ps{t}", nc.vector.tensor_copy)
 
         g_w = sb.tile([P, Q], U32, align_bytes=64)
         g_s = sb.tile([P, Q], U8, align_bytes=64)
@@ -165,19 +177,16 @@ def tile_list_ctxbeside_chosen_one_weighedout_kernel(
 
         for h in range(2):
             cols = slice(h * P, (h + 1) * P)
-            ph_ps = ps.tile([P, O], F32, name=f"ph_ps{h}")
+            ph_ps = ps.tile([P, O], F32, name=("bank_a", "bank_b")[h])
             nc.tensor.matmul_mx(out=ph_ps[:], lhsT=wb_w[:, cols].bitcast(E5M2), lhsT_scale=wb_s[:, cols],
                                 rhs=h_w[:].bitcast(E4M3), rhs_scale=h_s[:], start=True, stop=True)
             if h == 0:
                 nc.vector.tensor_copy(p_sb[h][:, 0:O], ph_ps[:])
             else:
                 nc.scalar.activation(p_sb[h][:, 0:O], ph_ps[:], COPY)
-        weighed = [sb.tile([P, U], F32, name=f"weighed{h}") for h in range(2)]
-        kept = [sb.tile([P, U], F32, name=f"kept{h}") for h in range(2)]
         for h in range(2):
-            nc.scalar.activation(weighed[h][:], p_sb[h][:].indirect(l6[:]), COPY, scale=so_t[:, h : h + 1])
-            nc.vector.tensor_copy(kept[h][:], p_sb[h][:].indirect(l5[:]))
-        for h in range(2):
+            weighed = sb.tile([P, U], F32, name=f"weighed{h}")
             y = sb.tile([P, U], F32, name=f"y{h}")
-            nc.vector.tensor_tensor(y[:], kept[h][:], weighed[h][:], ALU.subtract)
+            nc.scalar.activation(weighed[:], p_sb[h][:].indirect(l6[:]), COPY, scale=so_t[:, h : h + 1])
+            nc.vector.tensor_tensor(y[:], p_sb[h][:].indirect(l5[:]), weighed[:], ALU.subtract)
             (nc.scalar if h == 0 else nc.sync).dma_start(out[h * P : (h + 1) * P, :], y[:])

@@ -150,10 +150,9 @@ def tile_list_ctxbeside_chosen_one_weighedout_kernel(
         h_w = sb.tile([P, O], U32, align_bytes=64)
         h_s = sb.tile([P, O], U8, align_bytes=64)
 
-        def fetch(t, lo, hi):
-            cols = slice(lo // 16, hi // 16)
-            nc.scalar.activation(first[:, t, lo:hi], a[t][:].indirect(l3[:, cols]), COPY, scale=g0[:, t, 0:1])
-            nc.scalar.activation(second[:, t, lo:hi], a[t][:].indirect(l4[:, cols]), COPY, scale=g0[:, t, 64:65])
+        def fetch(dst, offsets, context, t, lo, hi):
+            nc.scalar.activation(dst[:, t, lo:hi], a[t][:].indirect(offsets[:, lo // 16 : hi // 16]), COPY,
+                                 scale=g0[:, t, context : context + 1])
 
         def larger(t, lo, hi):
             nc.vector.tensor_tensor(
@@ -163,13 +162,15 @@ def tile_list_ctxbeside_chosen_one_weighedout_kernel(
                 ALU.max,
             )
 
-        fetch(0, 0, O)
-        fetch(1, 0, O)
-        larger(0, 0, O)
+        for t in range(PACK - 1):
+            fetch(first, l3, 0, t, 0, O)
+            fetch(second, l4, 64, t, 0, O)
+            if t == 1:
+                larger(0, 0, O)
+        fetch(first, l3, 0, PACK - 1, 0, O)
         halves = [(0, O // 2), (O // 2, O)]
         for lo, hi in halves:
-            fetch(2, lo, hi)
-            fetch(3, lo, hi)
+            fetch(second, l4, 64, PACK - 1, lo, hi)
             larger(2, lo, hi)
         for lo, hi in halves:
             nc.vector.quantize_mx(out=h_w[:, lo:hi].bitcast(E4M3), scales=h_s[:, lo:hi],
@@ -188,5 +189,10 @@ def tile_list_ctxbeside_chosen_one_weighedout_kernel(
             weighed = sb.tile([P, U], F32, name=f"weighed{h}")
             y = sb.tile([P, U], F32, name=f"y{h}")
             nc.scalar.activation(weighed[:], p_sb[h][:].indirect(l6[:]), COPY, scale=so_t[:, h : h + 1])
-            nc.vector.tensor_tensor(y[:], p_sb[h][:].indirect(l5[:]), weighed[:], ALU.subtract)
+            if h == 0:
+                kept = sb.tile([P, U], F32)
+                nc.vector.tensor_copy(kept[:], p_sb[h][:].indirect(l5[:]))
+                nc.vector.tensor_tensor(y[:], kept[:], weighed[:], ALU.subtract)
+            else:
+                nc.vector.tensor_tensor(y[:], p_sb[h][:].indirect(l5[:]), weighed[:], ALU.subtract)
             (nc.scalar if h == 0 else nc.sync).dma_start(out[h * P : (h + 1) * P, :], y[:])

from contextlib import ExitStack

import concourse.mybir as mybir
from concourse.masks import make_identity

F32 = mybir.dt.float32
BF16 = mybir.dt.bfloat16
I32 = mybir.dt.int32
U32 = mybir.dt.uint32
U16 = mybir.dt.uint16
U8 = mybir.dt.uint8
E4M3 = mybir.dt.float8_e4m3fn_x4
E5M2 = mybir.dt.float8_e5m2_x4
E2M1 = mybir.dt.float4_e2m1fn_x4
COPY = mybir.ActivationFunctionType.Copy
ALU = mybir.AluOpType

P = 128
PACK = 4
T, J, R, V, Q, O, D, N, U = 1024, 256, 512, 1024, 128, 128, 256, 256, 128
FLOPS = 2 * 512 * (R * J + R * Q + N * D)


def tile_list_ctxbeside_chosen_one_weighedout_kernel(
    tc, xt_words, xt_scales, wt_words, wt_scales, xc_words, xc_scales, wg_words, wg_scales,
    wb_words, wb_scales, so, offs, offs2, offs3, offs4, offs5, offs6, out
):
    nc = tc.nc
    with ExitStack() as ctx:
        sb = ctx.enter_context(tc.tile_pool(name="sb", bufs=1))
        ps = ctx.enter_context(tc.psum_pool(name="ps", bufs=1))

        def load_list(name, src):
            tile = sb.tile(list(src.shape), U16, name=name)
            nc.sync.dma_start(tile[:], src)
            return tile

        def load_words(queue, name, src, dtype, cols):
            tile = sb.tile([P, cols], dtype, name=name, align_bytes=64)
            rows = src[0] if src.ndim == 3 else src[0].rearrange("p n t -> p (n t)")
            queue.dma_start(tile[:].bitcast(I32), rows.bitcast(I32))
            return tile

        def zeroed_plane(name, cols):
            tile = sb.tile([P, cols], U8, name=name, align_bytes=64)
            nc.vector.memset(tile[:].bitcast(I32), 0)
            return tile

        def load_scales(plane, src):
            rows = src[0].bitcast(I32)
            for quad in range(4):
                nc.sync.dma_start(plane[32 * quad : 32 * quad + 4, :].bitcast(I32), rows[4 * quad : 4 * quad + 4, :])

        g_plane = zeroed_plane("g_plane", R + Q)
        wt_s = zeroed_plane("wt_s", V)
        xt_s = zeroed_plane("xt_s", T)
        wb_s = zeroed_plane("wb_s", N)

        staged = sb.tile([4, 4, (R + Q) // 4], I32)
        nc.sync.dma_start(staged[:, :, 0 : R // 4], wg_scales[0].bitcast(I32).rearrange("(q r) c -> r q c", r=4))
        wt_w = load_words(nc.scalar, "wt_w", wt_words, U16, V)
        nc.sync.dma_start(staged[:, :, R // 4 :], xc_scales[0].bitcast(I32).rearrange("(q r) c -> r q c", r=4))
        wg_w = load_words(nc.scalar, "wg_w", wg_words, U16, R)
        l1 = load_list("l1", offs)
        xc_w = load_words(nc.scalar, "xc_w", xc_words, U32, Q)
        l2 = load_list("l2", offs2)
        xt_w = load_words(nc.scalar, "xt_w", xt_words, U32, T)
        load_scales(wt_s, wt_scales)
        load_scales(xt_s, xt_scales)
        l3 = load_list("l3", offs3)
        l4 = load_list("l4", offs4)
        wb_w = load_words(nc.sync, "wb_w", wb_words, U32, N)
        load_scales(wb_s, wb_scales)
        l5 = load_list("l5", offs5)
        l6 = load_list("l6", offs6)
        for quad in range(4):
            nc.vector.tensor_copy(g_plane[32 * quad : 32 * quad + 4, :].bitcast(I32), staged[:, quad, :])
        wg_s = g_plane[:, 0:R]
        xc_s = g_plane[:, R : R + Q]
        so_t = sb.tile([P, 2], F32)
        with nc.allow_non_contiguous_dma(reason="one weight a partition"):
            nc.sync.dma_start(so_t[:], so.rearrange("(h p) o -> p (h o)", p=P))

        ident = sb.tile([P, P], F32)
        make_identity(nc, ident[:])

        wt_gw = sb.tile([P, R], U16, align_bytes=64)
        nc.vector.tensor_copy(wt_gw[:], wt_w[:].indirect(l1[:]))
        xt_gw = sb.tile([P, J], U32, align_bytes=64)
        nc.vector.tensor_copy(xt_gw[:], xt_w[:].indirect(l2[:]))

        def deal(t, tag):
            tile = sb.tile([P, 2, P], U16, name=f"wt_dw{t}", tag=tag, align_bytes=64)
            nc.vector.tensor_copy(
                tile[:].rearrange("p t (c i) -> p c t i", i=8),
                wt_gw[:].rearrange("p (c i t) -> p c t i", i=8, t=PACK)[:, :, t : t + 2, :],
            )
            return [tile[:, 0, :], tile[:, 1, :]]

        wt_dw = deal(0, "wt_dw")
        wt_gs = sb.tile([P, PACK, P], U8, align_bytes=64)
        nc.vector.tensor_copy(wt_gs[:].rearrange("p t m -> p m t"), wt_s[:].indirect(l1[:]))
        xt_gs = sb.tile([P, J], U8, align_bytes=64)
        for lo in (0, J // 2):
            nc.vector.tensor_copy(xt_gs[:, lo : lo + J // 2], xt_s[:].indirect(l2[:, lo // 16 : (lo + J // 2) // 16]))

        wt_dw = wt_dw + deal(2, "xt_s")

        gT_ps = ps.tile([P, R], F32, tag="shared")
        nc.tensor.matmul_mx(out=gT_ps[:], lhsT=xc_w[:].bitcast(E4M3), lhsT_scale=xc_s,
                            rhs=wg_w[:].bitcast(E2M1), rhs_scale=wg_s, start=True, stop=True)
        gT = sb.tile([P, PACK, P], F32)
        nc.scalar.activation(gT[:], gT_ps[:].rearrange("q (m t) -> q t m", t=PACK), COPY)
        g_ps = ps.tile([P, PACK, Q], F32)
        for t in range(PACK):
            nc.tensor.transpose(g_ps[:, t, :], gT[:, t, :], ident[:])
        g0 = sb.tile([P, PACK, Q], F32)
        nc.scalar.activation(g0[:], g_ps[:], COPY)
        hid_g = sb.tile([P, Q, PACK], BF16, align_bytes=64)
        nc.scalar.activation(hid_g[:], g_ps[:].rearrange("p t q -> p q t"), COPY)

        a = [sb.tile([P, J], F32, name=f"a{t}") for t in range(PACK)]

        def hidden(t, lo, hi, bank, copy):
            a_ps = ps.tile([P, hi - lo], F32, name=bank)
            nc.tensor.matmul_mx(out=a_ps[:], lhsT=wt_dw[t].bitcast(E2M1), lhsT_scale=wt_gs[:, t, :],
                                rhs=xt_gw[:, lo:hi].bitcast(E4M3), rhs_scale=xt_gs[:, lo:hi], start=True, stop=True)
            copy(a[t][:, lo:hi], a_ps[:])

        hidden(0, 0, J // 2, "bank_a", nc.scalar.copy)
        hidden(0, J // 2, J, "bank_b", nc.vector.tensor_copy)
        for t in range(1, PACK):
            hidden(t, 0, J, f"a_ps{t}", nc.vector.tensor_copy)

        g_w = sb.tile([P, Q], U32, align_bytes=64)
        g_s = sb.tile([P, Q], U8, align_bytes=64)
        nc.vector.quantize_mx(out=g_w[:].bitcast(E4M3), scales=g_s[:], in_=hid_g[:].rearrange("p q t -> p (q t)"))
        p_sb = [sb.tile([P, D], F32, name=f"p{h}") for h in range(2)]
        pg_ps = ps.tile([P, 2, Q], F32, tag="shared")
        for h in range(2):
            cols = slice(h * P, (h + 1) * P)
            nc.tensor.matmul_mx(out=pg_ps[:, h, :], lhsT=wb_w[:, cols].bitcast(E5M2), lhsT_scale=wb_s[:, cols],
                                rhs=g_w[:].bitcast(E4M3), rhs_scale=g_s[:], start=True, stop=True)
        for h in range(2):
            nc.vector.tensor_copy(p_sb[h][:, O:D], pg_ps[:, h, :])

        first = sb.tile([P, PACK, O], F32)
        second = sb.tile([P, PACK, O], F32)
        hid_h = sb.tile([P, O, PACK], BF16, align_bytes=64)
        h_w = sb.tile([P, O], U32, align_bytes=64)
        h_s = sb.tile([P, O], U8, align_bytes=64)

        def fetch(dst, offsets, context, t, lo, hi):
            nc.scalar.activation(dst[:, t, lo:hi], a[t][:].indirect(offsets[:, lo // 16 : hi // 16]), COPY,
                                 scale=g0[:, t, context : context + 1])

        def larger(t, lo, hi):
            nc.vector.tensor_tensor(
                hid_h[:, lo:hi, t : t + 2],
                first[:, t : t + 2, lo:hi].rearrange("p t o -> p o t"),
                second[:, t : t + 2, lo:hi].rearrange("p t o -> p o t"),
                ALU.max,
            )

        for t in range(PACK - 1):
            fetch(first, l3, 0, t, 0, O)
            fetch(second, l4, 64, t, 0, O)
            if t == 1:
                larger(0, 0, O)
        fetch(first, l3, 0, PACK - 1, 0, O)
        halves = [(0, O // 2), (O // 2, O)]
        for lo, hi in halves:
            fetch(second, l4, 64, PACK - 1, lo, hi)
            larger(2, lo, hi)
        for lo, hi in halves:
            nc.vector.quantize_mx(out=h_w[:, lo:hi].bitcast(E4M3), scales=h_s[:, lo:hi],
                                  in_=hid_h[:, lo:hi, :].rearrange("p o t -> p (o t)"))

        for h in range(2):
            cols = slice(h * P, (h + 1) * P)
            ph_ps = ps.tile([P, O], F32, name=("bank_a", "bank_b")[h])
            nc.tensor.matmul_mx(out=ph_ps[:], lhsT=wb_w[:, cols].bitcast(E5M2), lhsT_scale=wb_s[:, cols],
                                rhs=h_w[:].bitcast(E4M3), rhs_scale=h_s[:], start=True, stop=True)
            if h == 0:
                nc.vector.tensor_copy(p_sb[h][:, 0:O], ph_ps[:])
            else:
                nc.scalar.activation(p_sb[h][:, 0:O], ph_ps[:], COPY)
        for h in range(2):
            weighed = sb.tile([P, U], F32, name=f"weighed{h}")
            y = sb.tile([P, U], F32, name=f"y{h}")
            nc.scalar.activation(weighed[:], p_sb[h][:].indirect(l6[:]), COPY, scale=so_t[:, h : h + 1])
            if h == 0:
                kept = sb.tile([P, U], F32)
                nc.vector.tensor_copy(kept[:], p_sb[h][:].indirect(l5[:]))
                nc.vector.tensor_tensor(y[:], kept[:], weighed[:], ALU.subtract)
            else:
                nc.vector.tensor_tensor(y[:], p_sb[h][:].indirect(l5[:]), weighed[:], ALU.subtract)
            (nc.scalar if h == 0 else nc.sync).dma_start(out[h * P : (h + 1) * P, :], y[:])
